import numpy as np
import ml_dtypes


def mxq(x, axis, fmt="e4m3"):
    dtype, down = {"e4m3": (ml_dtypes.float8_e4m3fn, 7), "e5m2": (ml_dtypes.float8_e5m2, 14)}[fmt]
    v = np.moveaxis(np.asarray(x, np.float32).astype(ml_dtypes.bfloat16).astype(np.float64), axis, -1)
    blocks = v.reshape(v.shape[:-1] + (-1, 32))
    amax = np.abs(blocks).max(-1, keepdims=True)
    byte = np.maximum(np.where(amax > 0, np.frexp(amax)[1] - 1 + 127, 0) - down, 1)
    scale = np.exp2(byte - 127.0)
    codes = (blocks / scale).astype(np.float32).astype(dtype).astype(np.float64)
    return np.moveaxis((codes * scale).reshape(v.shape), -1, axis)


WIDE = False


def mx_kscale(k):
    if not WIDE:
        return np.ones(k)
    levels = np.array([10, -10, 5, -5, 0])
    if k % 512:
        return np.exp2(np.random.permutation(np.resize(levels, k // 32))).repeat(32)
    a = np.empty((k // 512, 16))
    for p in range(k // 512):
        a[p, :8] = np.random.permutation(np.resize(levels, 8))
        for g in range(8):
            far = levels[np.abs(levels - a[p, g]) >= 10]
            a[p, g + 8] = far[np.random.randint(len(far))]
    return np.exp2(a.ravel()).repeat(32)


def f64(x):
    return np.asarray(x).astype(np.float64)


def striped(idx):
    return np.tile(np.asarray(idx).reshape(-1, 16).T, (8, 1)).astype(np.uint16)


def unstriped(offs):
    return offs[:16].T.reshape(-1).astype(np.int64)


E2M1 = np.array([0.0, 0.5, 1.0, 1.5, 2.0, 3.0, 4.0, 6.0, -0.0, -0.5, -1.0, -1.5, -2.0, -3.0, -4.0, -6.0])


def pack_weight(w, fmt):
    k, n = w.shape
    w = f64(np.asarray(w, np.float32).astype(ml_dtypes.bfloat16)).reshape(k // 32, 32, n)
    amax = np.abs(w).max(1)
    if fmt == "e4m3":
        byte = np.frexp(amax)[1] - 1 + 127 - 7
    else:
        mant, ex = np.frexp(amax / 6.0)
        byte = np.where(mant > 0.5, ex, ex - 1) + 127
    byte = np.clip(np.where(amax > 0, byte, 1), 1, 254)
    scaled = (w * np.exp2(127.0 - byte)[:, None, :]).reshape(k, n).astype(np.float32)
    by_word = np.ascontiguousarray(scaled.reshape(k // 512, 128, 4, n).transpose(0, 1, 3, 2))
    if fmt == "e4m3":
        words = by_word.astype(ml_dtypes.float8_e4m3fn).view(np.uint8)
    else:
        c = by_word.astype(ml_dtypes.float4_e2m1fn).view(np.uint8) & 0xF
        words = (c[..., 0::2] | (c[..., 1::2] << 4)).reshape(k // 512, 128, 2 * n)
    return np.ascontiguousarray(words), np.ascontiguousarray(byte.astype(np.uint8).reshape(k // 512, 16, n))


def unpack_weight(words, scales, fmt):
    g, _, n = scales.shape
    words = np.ascontiguousarray(words).reshape(g, 128, n, -1)
    if fmt == "e4m3":
        vals = words.view(ml_dtypes.float8_e4m3fn).astype(np.float64)
    else:
        nib = np.empty((g, 128, n, 4), np.uint8)
        nib[..., 0::2] = words & 0xF
        nib[..., 1::2] = words >> 4
        vals = E2M1[nib]
    vals = vals * np.repeat(np.exp2(scales.astype(np.float64) - 127.0), 8, axis=1)[..., None]
    return vals.transpose(0, 1, 3, 2).reshape(g * 512, n)


D, K, T, U, I, E = 512, 512, 2048, 1024, 512, 256


def setup_inputs():
    n = np.random.standard_normal
    idx = np.random.permutation(T)[:I]
    idx2 = np.random.permutation(U)[:I]
    fd = mx_kscale(D)
    fk = mx_kscale(K)
    pagesp = pack_weight(n((D, T)) / fd[:, None], "e2m1")
    wap = pack_weight(n((D, K)) * 1.0 / np.sqrt(D) * fd[:, None], "e4m3")
    notesp = pack_weight(n((D, U)) / fd[:, None], "e4m3")
    wbp = pack_weight(n((D, K)) * 1.0 / np.sqrt(D) * fd[:, None], "e2m1")
    wop = pack_weight(n((K, E)) * 1.0 / np.sqrt(K) / fk[:, None], "e4m3")
    wpp = pack_weight(n((K, E)) * 1.0 / np.sqrt(K) / fk[:, None], "e2m1")
    return {
        "pages_words": pagesp[0],
        "pages_scales": pagesp[1],
        "wa_words": wap[0],
        "wa_scales": wap[1],
        "notes_words": notesp[0],
        "notes_scales": notesp[1],
        "wb_words": wbp[0],
        "wb_scales": wbp[1],
        "kf": (np.random.uniform(0.5, 2.0, (K, 1)) * fk[:, None]).astype(np.float32),
        "kf2": (np.random.uniform(0.5, 2.0, (K, 1)) * fk[:, None]).astype(np.float32),
        "wo_words": wop[0],
        "wo_scales": wop[1],
        "wp_words": wpp[0],
        "wp_scales": wpp[1],
        "offs": striped(idx),
        "offs2": striped(idx2),
    }


def reference(pages_words, pages_scales, wa_words, wa_scales, notes_words, notes_scales, wb_words, wb_scales, kf, kf2, wo_words, wo_scales, wp_words, wp_scales, offs, offs2):
    idx = unstriped(offs)
    idx2 = unstriped(offs2)
    pagesu = unpack_weight(pages_words, pages_scales, "e2m1")
    wau = unpack_weight(wa_words, wa_scales, "e4m3")
    notesu = unpack_weight(notes_words, notes_scales, "e4m3")
    wbu = unpack_weight(wb_words, wb_scales, "e2m1")
    wou = unpack_weight(wo_words, wo_scales, "e4m3")
    wpu = unpack_weight(wp_words, wp_scales, "e2m1")
    pagesidxg = pagesu[:, idx]
    z = wau.T @ pagesidxg
    h1 = wbu.T @ notesu
    w = z * f64(kf)
    w2 = h1[:, idx2] * f64(kf2)
    wq = mxq(w, 0, "e4m3")
    w2q = mxq(w2, 0, "e4m3")
    y = wou.T @ wq + wpu.T @ w2q
    return y

@@ -1,0 +1,175 @@
+from contextlib import ExitStack
+
+import concourse.mybir as mybir
+
+D, K, T, U, I, E = 512, 512, 2048, 1024, 512, 256
+FLOPS = 2 * D * K * I + 2 * D * K * U + 2 * 2 * K * E * I
+
+F32 = mybir.dt.float32
+BF16 = mybir.dt.bfloat16
+I32 = mybir.dt.int32
+U32 = mybir.dt.uint32
+U16 = mybir.dt.uint16
+U8 = mybir.dt.uint8
+FP8X4 = mybir.dt.float8_e4m3fn_x4
+FP4X4 = mybir.dt.float4_e2m1fn_x4
+COPY = mybir.ActivationFunctionType.Copy
+MULT = mybir.AluOpType.mult
+
+P = 128
+PACK = 4
+BANK = 512
+HALF = I // 2
+
+
+def load_scales(queue, plane, scales):
+    for q in range(4):
+        queue.dma_start(
+            out=plane[32 * q : 32 * q + 4, :].bitcast(I32),
+            in_=scales[0, 4 * q : 4 * q + 4, :].bitcast(I32),
+        )
+
+
+def deal(engine, dealt, raw, run):
+    engine.tensor_copy(
+        out=dealt[:].rearrange("p (t c j) -> p c t j", t=PACK, j=run),
+        in_=raw.rearrange("p (c j t) -> p c t j", t=PACK, j=run),
+    )
+
+
+def tile_attend_pagesandhidden_kernel(
+    tc, pages_words, pages_scales, wa_words, wa_scales, notes_words, notes_scales, wb_words, wb_scales,
+    kf, kf2, wo_words, wo_scales, wp_words, wp_scales, offs, offs2, out,
+):
+    nc = tc.nc
+    with ExitStack() as ctx:
+        sb = ctx.enter_context(tc.tile_pool(name="sb", bufs=1))
+        ps = ctx.enter_context(tc.psum_pool(name="ps", bufs=1))
+
+        wb_raw = sb.tile([P, K], U16, align_bytes=64)
+        wb_s_raw = sb.tile([P, K], U8, align_bytes=64)
+        notes = sb.tile([P, U], U32, align_bytes=64)
+        notes_s = sb.tile([P, U], U8, align_bytes=64)
+        pages = sb.tile([P, T], U16, align_bytes=64)
+        pages_s = sb.tile([P, T], U8, align_bytes=64)
+        wa_raw = sb.tile([P, K], U32, align_bytes=64)
+        wa_s_raw = sb.tile([P, K], U8, align_bytes=64)
+        wo = sb.tile([P, E], U32, align_bytes=64)
+        wo_s = sb.tile([P, E], U8, align_bytes=64)
+        wp = sb.tile([P, E], U16, align_bytes=64)
+        wp_s = sb.tile([P, E], U8, align_bytes=64)
+        list1 = sb.tile([P, I // 16], U16)
+        list2 = sb.tile([P, I // 16], U16)
+        kf_sb = sb.tile([P, PACK], F32)
+        kf2_sb = sb.tile([P, PACK], F32)
+
+        for plane in (wb_s_raw, notes_s, pages_s, wa_s_raw, wo_s, wp_s):
+            nc.vector.memset(plane[:].bitcast(I32), 0)
+
+        load_scales(nc.sync, wb_s_raw, wb_scales)
+        nc.sync.dma_start(out=wb_raw[:].bitcast(I32), in_=wb_words[0].bitcast(I32))
+        nc.sync.dma_start(list1[:], offs)
+        nc.sync.dma_start(out=notes[:].bitcast(I32), in_=notes_words[0].rearrange("p n t -> p (n t)").bitcast(I32))
+        nc.sync.dma_start(out=pages[:].bitcast(I32), in_=pages_words[0].bitcast(I32))
+        load_scales(nc.sync, notes_s, notes_scales)
+        load_scales(nc.sync, pages_s, pages_scales)
+        nc.sync.dma_start(list2[:], offs2)
+        nc.sync.dma_start(out=wa_raw[:].bitcast(I32), in_=wa_words[0].rearrange("p n t -> p (n t)").bitcast(I32))
+        load_scales(nc.sync, wa_s_raw, wa_scales)
+        nc.sync.dma_start(out=kf_sb[:], in_=kf.rearrange("(p t) o -> p (t o)", t=PACK))
+        nc.sync.dma_start(out=kf2_sb[:], in_=kf2.rearrange("(p t) o -> p (t o)", t=PACK))
+        load_scales(nc.sync, wo_s, wo_scales)
+        load_scales(nc.sync, wp_s, wp_scales)
+        nc.sync.dma_start(out=wo[:].bitcast(I32), in_=wo_words[0].rearrange("p n t -> p (n t)").bitcast(I32))
+        nc.sync.dma_start(out=wp[:].bitcast(I32), in_=wp_words[0].bitcast(I32))
+
+        wb = sb.tile([P, K], U16, align_bytes=64)
+        wb_s = sb.tile([P, K], U8, align_bytes=64)
+        deal(nc.vector, wb_s, wb_s_raw[:], 16)
+        deal(nc.vector, wb, wb_raw[:], 8)
+
+        h1 = [sb.tile([P, U], F32, name=f"h1_{t}") for t in range(PACK)]
+        for t in range(PACK):
+            cols = slice(t * P, (t + 1) * P)
+            for u0 in range(0, U, BANK):
+                bank = ps.tile([P, BANK], F32, name="h_bank", tag="wide", bufs=4)
+                nc.tensor.matmul_mx(
+                    out=bank[:], lhsT=wb[:, cols].bitcast(FP4X4), lhsT_scale=wb_s[:, cols],
+                    rhs=notes[:, u0 : u0 + BANK].bitcast(FP8X4), rhs_scale=notes_s[:, u0 : u0 + BANK],
+                    start=True, stop=True,
+                )
+                nc.scalar.activation(h1[t][:, u0 : u0 + BANK], bank[:], COPY)
+
+        picked = sb.tile([P, I], U16, align_bytes=64)
+        picked_s = sb.tile([P, I], U8, align_bytes=64)
+        nc.vector.tensor_copy(picked[:], pages[:].indirect(list1[:]))
+        nc.vector.tensor_copy(picked_s[:], pages_s[:].indirect(list1[:]))
+        wa = sb.tile([P, K], U32, align_bytes=64)
+        wa_s = sb.tile([P, K], U8, align_bytes=64)
+        deal(nc.gpsimd, wa_s, wa_s_raw[:], 16)
+        deal(nc.gpsimd, wa, wa_raw[:], 4)
+
+        found = [sb.tile([P, PACK, HALF], F32, name=f"found{h}") for h in range(2)]
+        halves = [list2[:, h * HALF // 16 : (h + 1) * HALF // 16] for h in range(2)]
+        on_vector = [(0, 0), (1, 0), (0, 1)]
+        for h, t in on_vector[:2]:
+            nc.vector.tensor_copy(found[h][:, t, :], h1[t][:].indirect(halves[h]))
+
+        w = sb.tile([P, I, PACK], BF16, align_bytes=64)
+        for i0 in range(0, I, P):
+            bank = ps.tile([P, PACK, P], F32, name="z_bank", bufs=4)
+            for t in range(PACK):
+                cols = slice(t * P, (t + 1) * P)
+                nc.tensor.matmul_mx(
+                    out=bank[:, t, :], lhsT=wa[:, cols].bitcast(FP8X4), lhsT_scale=wa_s[:, cols],
+                    rhs=picked[:, i0 : i0 + P].bitcast(FP4X4), rhs_scale=picked_s[:, i0 : i0 + P],
+                    start=True, stop=True,
+                )
+            nc.vector.tensor_tensor(
+                w[:, i0 : i0 + P, :], bank[:].rearrange("p t n -> p n t"),
+                kf_sb[:].unsqueeze(1).broadcast_to([P, P, PACK]), MULT,
+            )
+        wq = sb.tile([P, I], U32, align_bytes=64)
+        wq_s = sb.tile([P, I], U8, align_bytes=64)
+        nc.vector.quantize_mx(out=wq[:].bitcast(FP8X4), scales=wq_s[:], in_=w[:].rearrange("p n t -> p (n t)"))
+
+        sums = [[ps.tile([P, HALF], F32, name=f"sum{h}{e}", tag="wide", bufs=4) for e in range(2)] for h in range(2)]
+        for h in range(2):
+            slots = slice(h * HALF, (h + 1) * HALF)
+            for e in range(2):
+                cols = slice(e * P, (e + 1) * P)
+                nc.tensor.matmul_mx(
+                    out=sums[h][e][:], lhsT=wo[:, cols].bitcast(FP8X4), lhsT_scale=wo_s[:, cols],
+                    rhs=wq[:, slots].bitcast(FP8X4), rhs_scale=wq_s[:, slots], start=True, stop=False,
+                )
+
+        for h, t in on_vector[2:]:
+            nc.vector.tensor_copy(found[h][:, t, :], h1[t][:].indirect(halves[h]))
+        for h in range(2):
+            for t in range(PACK):
+                if (h, t) not in on_vector:
+                    nc.scalar.activation(found[h][:, t, :], h1[t][:].indirect(halves[h]), COPY)
+
+        for h in range(2):
+            slots = slice(h * HALF, (h + 1) * HALF)
+            w2 = sb.tile([P, HALF, PACK], BF16, name=f"w2_{h}", align_bytes=64)
+            nc.vector.tensor_tensor(
+                w2[:], found[h][:].rearrange("p t n -> p n t"),
+                kf2_sb[:].unsqueeze(1).broadcast_to([P, HALF, PACK]), MULT,
+            )
+            w2q = sb.tile([P, HALF], U32, name=f"w2q_{h}", align_bytes=64)
+            w2q_s = sb.tile([P, HALF], U8, name=f"w2q_s_{h}", align_bytes=64)
+            nc.vector.quantize_mx(out=w2q[:].bitcast(FP8X4), scales=w2q_s[:], in_=w2[:].rearrange("p n t -> p (n t)"))
+            for e in range(2):
+                cols = slice(e * P, (e + 1) * P)
+                nc.tensor.matmul_mx(
+                    out=sums[h][e][:], lhsT=wp[:, cols].bitcast(FP4X4), lhsT_scale=wp_s[:, cols],
+                    rhs=w2q[:].bitcast(FP8X4), rhs_scale=w2q_s[:], start=False, stop=True,
+                )
+                res = sb.tile([P, HALF], F32, name=f"res{h}{e}")
+                if h == 1 and e == 1:
+                    nc.vector.tensor_copy(res[:], sums[h][e][:])
+                    nc.sync.dma_start(out=out[cols, slots], in_=res[:])
+                else:
+                    nc.scalar.copy(res[:], sums[h][e][:])
+                    (nc.scalar if h == 1 else nc.sync).dma_start(out=out[cols, slots], in_=res[:])

@@ -22,11 +22,20 @@ BANK = 512
 HALF = I // 2
 
 
-def load_scales(queue, plane, scales):
-    for q in range(4):
+def load_scales(queue, plane, scales, quadrants=(0, 1, 2, 3)):
+    for q in quadrants:
         queue.dma_start(
             out=plane[32 * q : 32 * q + 4, :].bitcast(I32),
             in_=scales[0, 4 * q : 4 * q + 4, :].bitcast(I32),
+        )
+
+
+def fill_scales(queue, plane, scales, quadrants=(0, 1, 2, 3)):
+    for q in quadrants:
+        rows = scales[0, 4 * q : 4 * q + 4, :].bitcast(I32)
+        queue.dma_start(
+            out=plane[32 * q : 32 * q + 32, :].bitcast(I32),
+            in_=rows.unsqueeze(0).broadcast_to([8, 4, rows.shape[1]]),
         )
 
 
@@ -63,24 +72,25 @@ def tile_attend_pagesandhidden_kernel(
         kf_sb = sb.tile([P, PACK], F32)
         kf2_sb = sb.tile([P, PACK], F32)
 
-        for plane in (wb_s_raw, notes_s, pages_s, wa_s_raw, wo_s, wp_s):
+        for plane in (pages_s, wa_s_raw, wo_s, wp_s):
             nc.vector.memset(plane[:].bitcast(I32), 0)
 
-        load_scales(nc.sync, wb_s_raw, wb_scales)
+        fill_scales(nc.scalar, wb_s_raw, wb_scales)
         nc.sync.dma_start(out=wb_raw[:].bitcast(I32), in_=wb_words[0].bitcast(I32))
-        nc.sync.dma_start(list1[:], offs)
+        fill_scales(nc.sync, notes_s, notes_scales, (0,))
         nc.sync.dma_start(out=notes[:].bitcast(I32), in_=notes_words[0].rearrange("p n t -> p (n t)").bitcast(I32))
+        fill_scales(nc.sync, notes_s, notes_scales, (1, 2, 3))
         nc.sync.dma_start(out=pages[:].bitcast(I32), in_=pages_words[0].bitcast(I32))
-        load_scales(nc.sync, notes_s, notes_scales)
+        nc.sync.dma_start(list1[:], offs)
         load_scales(nc.sync, pages_s, pages_scales)
-        nc.sync.dma_start(list2[:], offs2)
         nc.sync.dma_start(out=wa_raw[:].bitcast(I32), in_=wa_words[0].rearrange("p n t -> p (n t)").bitcast(I32))
         load_scales(nc.sync, wa_s_raw, wa_scales)
-        nc.sync.dma_start(out=kf_sb[:], in_=kf.rearrange("(p t) o -> p (t o)", t=PACK))
-        nc.sync.dma_start(out=kf2_sb[:], in_=kf2.rearrange("(p t) o -> p (t o)", t=PACK))
+        nc.sync.dma_start(list2[:], offs2)
+        nc.gpsimd.dma_start(out=kf_sb[:], in_=kf.rearrange("(p t) o -> p (t o)", t=PACK))
+        nc.gpsimd.dma_start(out=kf2_sb[:], in_=kf2.rearrange("(p t) o -> p (t o)", t=PACK))
         load_scales(nc.sync, wo_s, wo_scales)
-        load_scales(nc.sync, wp_s, wp_scales)
         nc.sync.dma_start(out=wo[:].bitcast(I32), in_=wo_words[0].rearrange("p n t -> p (n t)").bitcast(I32))
+        load_scales(nc.sync, wp_s, wp_scales)
         nc.sync.dma_start(out=wp[:].bitcast(I32), in_=wp_words[0].bitcast(I32))
 
         wb = sb.tile([P, K], U16, align_bytes=64)
@@ -106,14 +116,16 @@ def tile_attend_pagesandhidden_kernel(
         nc.vector.tensor_copy(picked_s[:], pages_s[:].indirect(list1[:]))
         wa = sb.tile([P, K], U32, align_bytes=64)
         wa_s = sb.tile([P, K], U8, align_bytes=64)
-        deal(nc.gpsimd, wa_s, wa_s_raw[:], 16)
-        deal(nc.gpsimd, wa, wa_raw[:], 4)
+        deal(nc.vector, wa_s, wa_s_raw[:], 16)
+        deal(nc.vector, wa, wa_raw[:], 4)
 
-        found = [sb.tile([P, PACK, HALF], F32, name=f"found{h}") for h in range(2)]
-        halves = [list2[:, h * HALF // 16 : (h + 1) * HALF // 16] for h in range(2)]
-        on_vector = [(0, 0), (1, 0), (0, 1)]
-        for h, t in on_vector[:2]:
-            nc.vector.tensor_copy(found[h][:, t, :], h1[t][:].indirect(halves[h]))
+        pieces = [slice(0, 256), slice(256, 384), slice(384, 512)]
+        widths = [piece.stop - piece.start for piece in pieces]
+        found = [sb.tile([P, PACK, n], F32, name=f"found{h}") for h, n in enumerate(widths)]
+        windows = [
+            [h1[t][:].indirect(list2[:, piece.start // 16 : piece.stop // 16]) for t in range(PACK)] for piece in pieces
+        ]
+        nc.vector.tensor_copy(found[0][:, 0, :], windows[0][0])
 
         w = sb.tile([P, I, PACK], BF16, align_bytes=64)
         for i0 in range(0, I, P):
@@ -133,43 +145,36 @@ def tile_attend_pagesandhidden_kernel(
         wq_s = sb.tile([P, I], U8, align_bytes=64)
         nc.vector.quantize_mx(out=wq[:].bitcast(FP8X4), scales=wq_s[:], in_=w[:].rearrange("p n t -> p (n t)"))
 
-        sums = [[ps.tile([P, HALF], F32, name=f"sum{h}{e}", tag="wide", bufs=4) for e in range(2)] for h in range(2)]
-        for h in range(2):
-            slots = slice(h * HALF, (h + 1) * HALF)
+        sums = [ps.tile([P, 2, n], F32, name=f"sum{h}", tag="wide", bufs=4) for h, n in enumerate(widths)]
+        for h, piece in enumerate(pieces):
             for e in range(2):
                 cols = slice(e * P, (e + 1) * P)
                 nc.tensor.matmul_mx(
-                    out=sums[h][e][:], lhsT=wo[:, cols].bitcast(FP8X4), lhsT_scale=wo_s[:, cols],
-                    rhs=wq[:, slots].bitcast(FP8X4), rhs_scale=wq_s[:, slots], start=True, stop=False,
+                    out=sums[h][:, e, :], lhsT=wo[:, cols].bitcast(FP8X4), lhsT_scale=wo_s[:, cols],
+                    rhs=wq[:, piece].bitcast(FP8X4), rhs_scale=wq_s[:, piece], start=(e == 0), stop=False,
                 )
 
-        for h, t in on_vector[2:]:
-            nc.vector.tensor_copy(found[h][:, t, :], h1[t][:].indirect(halves[h]))
-        for h in range(2):
+        for h in range(len(pieces)):
             for t in range(PACK):
-                if (h, t) not in on_vector:
-                    nc.scalar.activation(found[h][:, t, :], h1[t][:].indirect(halves[h]), COPY)
+                if (h, t) != (0, 0):
+                    nc.scalar.activation(found[h][:, t, :], windows[h][t], COPY)
 
-        for h in range(2):
-            slots = slice(h * HALF, (h + 1) * HALF)
-            w2 = sb.tile([P, HALF, PACK], BF16, name=f"w2_{h}", align_bytes=64)
+        for h, piece in enumerate(pieces):
+            n = widths[h]
+            w2 = sb.tile([P, n, PACK], BF16, name=f"w2_{h}", align_bytes=64)
             nc.vector.tensor_tensor(
-                w2[:], found[h][:].rearrange("p t n -> p n t"),
-                kf2_sb[:].unsqueeze(1).broadcast_to([P, HALF, PACK]), MULT,
+                w2[:].rearrange("p (c j) t -> p c t j", j=4), found[h][:].rearrange("p t (c j) -> p c t j", j=4),
+                kf2_sb[:].unsqueeze(1).unsqueeze(3).broadcast_to([P, n // 4, PACK, 4]), MULT,
             )
-            w2q = sb.tile([P, HALF], U32, name=f"w2q_{h}", align_bytes=64)
-            w2q_s = sb.tile([P, HALF], U8, name=f"w2q_s_{h}", align_bytes=64)
+            w2q = sb.tile([P, n], U32, name=f"w2q_{h}", align_bytes=64)
+            w2q_s = sb.tile([P, n], U8, name=f"w2q_s_{h}", align_bytes=64)
             nc.vector.quantize_mx(out=w2q[:].bitcast(FP8X4), scales=w2q_s[:], in_=w2[:].rearrange("p n t -> p (n t)"))
             for e in range(2):
                 cols = slice(e * P, (e + 1) * P)
                 nc.tensor.matmul_mx(
-                    out=sums[h][e][:], lhsT=wp[:, cols].bitcast(FP4X4), lhsT_scale=wp_s[:, cols],
-                    rhs=w2q[:].bitcast(FP8X4), rhs_scale=w2q_s[:], start=False, stop=True,
+                    out=sums[h][:, e, :], lhsT=wp[:, cols].bitcast(FP4X4), lhsT_scale=wp_s[:, cols],
+                    rhs=w2q[:].bitcast(FP8X4), rhs_scale=w2q_s[:], start=False, stop=(e == 1),
                 )
-                res = sb.tile([P, HALF], F32, name=f"res{h}{e}")
-                if h == 1 and e == 1:
-                    nc.vector.tensor_copy(res[:], sums[h][e][:])
-                    nc.sync.dma_start(out=out[cols, slots], in_=res[:])
-                else:
-                    nc.scalar.copy(res[:], sums[h][e][:])
-                    (nc.scalar if h == 1 else nc.sync).dma_start(out=out[cols, slots], in_=res[:])
+            res = sb.tile([P, 2, n], F32, name=f"res{h}")
+            nc.scalar.copy(res[:], sums[h][:])
+            nc.sync.dma_start(out=out[:, piece].rearrange("(e p) n -> p e n", p=P), in_=res[:])

@@ -15,6 +15,7 @@ FP8X4 = mybir.dt.float8_e4m3fn_x4
 FP4X4 = mybir.dt.float4_e2m1fn_x4
 COPY = mybir.ActivationFunctionType.Copy
 MULT = mybir.AluOpType.mult
+ADD = mybir.AluOpType.add
 
 P = 128
 PACK = 4
@@ -116,8 +117,8 @@ def tile_attend_pagesandhidden_kernel(
         nc.vector.tensor_copy(picked_s[:], pages_s[:].indirect(list1[:]))
         wa = sb.tile([P, K], U32, align_bytes=64)
         wa_s = sb.tile([P, K], U8, align_bytes=64)
-        deal(nc.vector, wa_s, wa_s_raw[:], 16)
-        deal(nc.vector, wa, wa_raw[:], 4)
+        deal(nc.gpsimd, wa, wa_raw[:], 4)
+        deal(nc.gpsimd, wa_s, wa_s_raw[:], 16)
 
         pieces = [slice(0, 256), slice(256, 384), slice(384, 512)]
         widths = [piece.stop - piece.start for piece in pieces]
@@ -125,10 +126,14 @@ def tile_attend_pagesandhidden_kernel(
         windows = [
             [h1[t][:].indirect(list2[:, piece.start // 16 : piece.stop // 16]) for t in range(PACK)] for piece in pieces
         ]
-        nc.vector.tensor_copy(found[0][:, 0, :], windows[0][0])
+        for h in range(len(pieces)):
+            nc.vector.tensor_copy(found[h][:, 0, :], windows[h][0])
 
-        w = sb.tile([P, I, PACK], BF16, align_bytes=64)
-        for i0 in range(0, I, P):
+        wq = sb.tile([P, I], U32, align_bytes=64)
+        wq_s = sb.tile([P, I], U8, align_bytes=64)
+        w = [sb.tile([P, HALF, PACK], BF16, name=f"w{g}", tag=f"rounded{g}", align_bytes=64) for g in range(2)]
+
+        def page_slots(i0):
             bank = ps.tile([P, PACK, P], F32, name="z_bank", bufs=4)
             for t in range(PACK):
                 cols = slice(t * P, (t + 1) * P)
@@ -138,12 +143,22 @@ def tile_attend_pagesandhidden_kernel(
                     start=True, stop=True,
                 )
             nc.vector.tensor_tensor(
-                w[:, i0 : i0 + P, :], bank[:].rearrange("p t n -> p n t"),
+                w[i0 // HALF][:, i0 % HALF : i0 % HALF + P, :], bank[:].rearrange("p t n -> p n t"),
                 kf_sb[:].unsqueeze(1).broadcast_to([P, P, PACK]), MULT,
             )
-        wq = sb.tile([P, I], U32, align_bytes=64)
-        wq_s = sb.tile([P, I], U8, align_bytes=64)
-        nc.vector.quantize_mx(out=wq[:].bitcast(FP8X4), scales=wq_s[:], in_=w[:].rearrange("p n t -> p (n t)"))
+
+        def quantise_pages(g):
+            slots = slice(g * HALF, (g + 1) * HALF)
+            nc.vector.quantize_mx(
+                out=wq[:, slots].bitcast(FP8X4), scales=wq_s[:, slots], in_=w[g][:].rearrange("p n t -> p (n t)")
+            )
+
+        page_slots(0)
+        page_slots(P)
+        page_slots(2 * P)
+        quantise_pages(0)
+        page_slots(3 * P)
+        quantise_pages(1)
 
         sums = [ps.tile([P, 2, n], F32, name=f"sum{h}", tag="wide", bufs=4) for h, n in enumerate(widths)]
         for h, piece in enumerate(pieces):
@@ -155,17 +170,25 @@ def tile_attend_pagesandhidden_kernel(
                 )
 
         for h in range(len(pieces)):
-            for t in range(PACK):
-                if (h, t) != (0, 0):
-                    nc.scalar.activation(found[h][:, t, :], windows[h][t], COPY)
+            for t in range(1, PACK):
+                nc.scalar.activation(found[h][:, t, :], windows[h][t], COPY)
+
+        scaled = [sb.tile([P, PACK, n], BF16, name=f"scaled{h}") for h, n in enumerate(widths[:2])]
+        for t, h in [(0, 0), (0, 1), (1, 0), (2, 0), (3, 0), (1, 1), (2, 1), (3, 1)]:
+            nc.gpsimd.tensor_scalar(scaled[h][:, t, :], found[h][:, t, :], kf2_sb[:, t : t + 1], 0.0, MULT, ADD)
 
         for h, piece in enumerate(pieces):
             n = widths[h]
-            w2 = sb.tile([P, n, PACK], BF16, name=f"w2_{h}", align_bytes=64)
-            nc.vector.tensor_tensor(
-                w2[:].rearrange("p (c j) t -> p c t j", j=4), found[h][:].rearrange("p t (c j) -> p c t j", j=4),
-                kf2_sb[:].unsqueeze(1).unsqueeze(3).broadcast_to([P, n // 4, PACK, 4]), MULT,
-            )
+            w2 = sb.tile([P, n, PACK], BF16, name=f"w2_{h}", tag=f"rounded{min(h, 1)}", align_bytes=64)
+            if h < 2:
+                nc.vector.tensor_copy(
+                    w2[:].rearrange("p (c j) t -> p c t j", j=4), scaled[h][:].rearrange("p t (c j) -> p c t j", j=4)
+                )
+            else:
+                nc.vector.tensor_tensor(
+                    w2[:].rearrange("p (c j) t -> p c t j", j=4), found[h][:].rearrange("p t (c j) -> p c t j", j=4),
+                    kf2_sb[:].unsqueeze(1).unsqueeze(3).broadcast_to([P, n // 4, PACK, 4]), MULT,
+                )
             w2q = sb.tile([P, n], U32, name=f"w2q_{h}", align_bytes=64)
             w2q_s = sb.tile([P, n], U8, name=f"w2q_s_{h}", align_bytes=64)
             nc.vector.quantize_mx(out=w2q[:].bitcast(FP8X4), scales=w2q_s[:], in_=w2[:].rearrange("p n t -> p (n t)"))
@@ -176,5 +199,8 @@ def tile_attend_pagesandhidden_kernel(
                     rhs=w2q[:].bitcast(FP8X4), rhs_scale=w2q_s[:], start=False, stop=(e == 1),
                 )
             res = sb.tile([P, 2, n], F32, name=f"res{h}")
-            nc.scalar.copy(res[:], sums[h][:])
+            if h < 2:
+                nc.scalar.copy(res[:], sums[h][:])
+            else:
+                nc.vector.tensor_copy(res[:], sums[h][:])
             nc.sync.dma_start(out=out[:, piece].rearrange("(e p) n -> p e n", p=P), in_=res[:])

@@ -19,31 +19,41 @@ ADD = mybir.AluOpType.add
 
 P = 128
 PACK = 4
+QUADRANTS = 4
 BANK = 512
+BANKS = 8
 HALF = I // 2
+LINE = 16
+PER_COLUMN = 16
+PIECES = (slice(0, 256), slice(256, 384), slice(384, 512))
 
 
-def load_scales(queue, plane, scales, quadrants=(0, 1, 2, 3)):
-    for q in quadrants:
+def load_scales(queue, plane, scales):
+    for q in range(QUADRANTS):
         queue.dma_start(
             out=plane[32 * q : 32 * q + 4, :].bitcast(I32),
             in_=scales[0, 4 * q : 4 * q + 4, :].bitcast(I32),
         )
 
 
-def fill_scales(queue, plane, scales, quadrants=(0, 1, 2, 3)):
+def fill_scales(queue, plane, scales, quadrants):
     for q in quadrants:
         rows = scales[0, 4 * q : 4 * q + 4, :].bitcast(I32)
         queue.dma_start(
             out=plane[32 * q : 32 * q + 32, :].bitcast(I32),
-            in_=rows.unsqueeze(0).broadcast_to([8, 4, rows.shape[1]]),
+            in_=rows.unsqueeze(0).broadcast_to([32 // 4, 4, rows.shape[1]]),
         )
 
 
-def deal(engine, dealt, raw, run):
+def load_words(nc, tile, words):
+    nc.sync.dma_start(out=tile[:].bitcast(I32), in_=words.bitcast(I32))
+
+
+def deal(engine, dealt, raw, element_bytes):
+    run = LINE // element_bytes
     engine.tensor_copy(
         out=dealt[:].rearrange("p (t c j) -> p c t j", t=PACK, j=run),
-        in_=raw.rearrange("p (c j t) -> p c t j", t=PACK, j=run),
+        in_=raw[:].rearrange("p (c j t) -> p c t j", t=PACK, j=run),
     )
 
 
@@ -68,48 +78,48 @@ def tile_attend_pagesandhidden_kernel(
         wo_s = sb.tile([P, E], U8, align_bytes=64)
         wp = sb.tile([P, E], U16, align_bytes=64)
         wp_s = sb.tile([P, E], U8, align_bytes=64)
-        list1 = sb.tile([P, I // 16], U16)
-        list2 = sb.tile([P, I // 16], U16)
+        list1 = sb.tile([P, I // PER_COLUMN], U16)
+        list2 = sb.tile([P, I // PER_COLUMN], U16)
         kf_sb = sb.tile([P, PACK], F32)
         kf2_sb = sb.tile([P, PACK], F32)
 
         for plane in (pages_s, wa_s_raw, wo_s, wp_s):
             nc.vector.memset(plane[:].bitcast(I32), 0)
 
-        fill_scales(nc.scalar, wb_s_raw, wb_scales)
-        nc.sync.dma_start(out=wb_raw[:].bitcast(I32), in_=wb_words[0].bitcast(I32))
-        fill_scales(nc.sync, notes_s, notes_scales, (0,))
-        nc.sync.dma_start(out=notes[:].bitcast(I32), in_=notes_words[0].rearrange("p n t -> p (n t)").bitcast(I32))
-        fill_scales(nc.sync, notes_s, notes_scales, (1, 2, 3))
-        nc.sync.dma_start(out=pages[:].bitcast(I32), in_=pages_words[0].bitcast(I32))
+        fill_scales(nc.scalar, wb_s_raw, wb_scales, range(QUADRANTS))
+        load_words(nc, wb_raw, wb_words[0])
+        fill_scales(nc.sync, notes_s, notes_scales, range(1))
+        load_words(nc, notes, notes_words[0].rearrange("p n t -> p (n t)"))
+        fill_scales(nc.sync, notes_s, notes_scales, range(1, QUADRANTS))
+        load_words(nc, pages, pages_words[0])
         nc.sync.dma_start(list1[:], offs)
         load_scales(nc.sync, pages_s, pages_scales)
-        nc.sync.dma_start(out=wa_raw[:].bitcast(I32), in_=wa_words[0].rearrange("p n t -> p (n t)").bitcast(I32))
+        load_words(nc, wa_raw, wa_words[0].rearrange("p n t -> p (n t)"))
         load_scales(nc.sync, wa_s_raw, wa_scales)
         nc.sync.dma_start(list2[:], offs2)
         nc.gpsimd.dma_start(out=kf_sb[:], in_=kf.rearrange("(p t) o -> p (t o)", t=PACK))
         nc.gpsimd.dma_start(out=kf2_sb[:], in_=kf2.rearrange("(p t) o -> p (t o)", t=PACK))
         load_scales(nc.sync, wo_s, wo_scales)
-        nc.sync.dma_start(out=wo[:].bitcast(I32), in_=wo_words[0].rearrange("p n t -> p (n t)").bitcast(I32))
+        load_words(nc, wo, wo_words[0].rearrange("p n t -> p (n t)"))
         load_scales(nc.sync, wp_s, wp_scales)
-        nc.sync.dma_start(out=wp[:].bitcast(I32), in_=wp_words[0].bitcast(I32))
+        load_words(nc, wp, wp_words[0])
 
         wb = sb.tile([P, K], U16, align_bytes=64)
         wb_s = sb.tile([P, K], U8, align_bytes=64)
-        deal(nc.vector, wb_s, wb_s_raw[:], 16)
-        deal(nc.vector, wb, wb_raw[:], 8)
+        deal(nc.vector, wb_s, wb_s_raw, 1)
+        deal(nc.vector, wb, wb_raw, 2)
 
         h1 = [sb.tile([P, U], F32, name=f"h1_{t}") for t in range(PACK)]
         for t in range(PACK):
             cols = slice(t * P, (t + 1) * P)
             for u0 in range(0, U, BANK):
-                bank = ps.tile([P, BANK], F32, name="h_bank", tag="wide", bufs=4)
+                h_bank = ps.tile([P, BANK], F32, tag="bank", bufs=BANKS)
                 nc.tensor.matmul_mx(
-                    out=bank[:], lhsT=wb[:, cols].bitcast(FP4X4), lhsT_scale=wb_s[:, cols],
+                    out=h_bank[:], lhsT=wb[:, cols].bitcast(FP4X4), lhsT_scale=wb_s[:, cols],
                     rhs=notes[:, u0 : u0 + BANK].bitcast(FP8X4), rhs_scale=notes_s[:, u0 : u0 + BANK],
                     start=True, stop=True,
                 )
-                nc.scalar.activation(h1[t][:, u0 : u0 + BANK], bank[:], COPY)
+                nc.scalar.activation(h1[t][:, u0 : u0 + BANK], h_bank[:], COPY)
 
         picked = sb.tile([P, I], U16, align_bytes=64)
         picked_s = sb.tile([P, I], U8, align_bytes=64)
@@ -117,33 +127,34 @@ def tile_attend_pagesandhidden_kernel(
         nc.vector.tensor_copy(picked_s[:], pages_s[:].indirect(list1[:]))
         wa = sb.tile([P, K], U32, align_bytes=64)
         wa_s = sb.tile([P, K], U8, align_bytes=64)
-        deal(nc.gpsimd, wa, wa_raw[:], 4)
-        deal(nc.gpsimd, wa_s, wa_s_raw[:], 16)
+        deal(nc.gpsimd, wa, wa_raw, 4)
+        deal(nc.gpsimd, wa_s, wa_s_raw, 1)
 
-        pieces = [slice(0, 256), slice(256, 384), slice(384, 512)]
-        widths = [piece.stop - piece.start for piece in pieces]
+        widths = [piece.stop - piece.start for piece in PIECES]
+        last = len(PIECES) - 1
         found = [sb.tile([P, PACK, n], F32, name=f"found{h}") for h, n in enumerate(widths)]
-        windows = [
-            [h1[t][:].indirect(list2[:, piece.start // 16 : piece.stop // 16]) for t in range(PACK)] for piece in pieces
+        listed = [
+            [h1[t][:].indirect(list2[:, piece.start // PER_COLUMN : piece.stop // PER_COLUMN]) for t in range(PACK)]
+            for piece in PIECES
         ]
-        for h in range(len(pieces)):
-            nc.vector.tensor_copy(found[h][:, 0, :], windows[h][0])
+        for h in range(len(PIECES)):
+            nc.vector.tensor_copy(found[h][:, 0, :], listed[h][0])
 
         wq = sb.tile([P, I], U32, align_bytes=64)
         wq_s = sb.tile([P, I], U8, align_bytes=64)
         w = [sb.tile([P, HALF, PACK], BF16, name=f"w{g}", tag=f"rounded{g}", align_bytes=64) for g in range(2)]
 
         def page_slots(i0):
-            bank = ps.tile([P, PACK, P], F32, name="z_bank", bufs=4)
+            z_bank = ps.tile([P, PACK, P], F32, tag="bank", bufs=BANKS)
             for t in range(PACK):
                 cols = slice(t * P, (t + 1) * P)
                 nc.tensor.matmul_mx(
-                    out=bank[:, t, :], lhsT=wa[:, cols].bitcast(FP8X4), lhsT_scale=wa_s[:, cols],
+                    out=z_bank[:, t, :], lhsT=wa[:, cols].bitcast(FP8X4), lhsT_scale=wa_s[:, cols],
                     rhs=picked[:, i0 : i0 + P].bitcast(FP4X4), rhs_scale=picked_s[:, i0 : i0 + P],
                     start=True, stop=True,
                 )
             nc.vector.tensor_tensor(
-                w[i0 // HALF][:, i0 % HALF : i0 % HALF + P, :], bank[:].rearrange("p t n -> p n t"),
+                w[i0 // HALF][:, i0 % HALF : i0 % HALF + P, :], z_bank[:].rearrange("p t n -> p n t"),
                 kf_sb[:].unsqueeze(1).broadcast_to([P, P, PACK]), MULT,
             )
 
@@ -160,46 +171,46 @@ def tile_attend_pagesandhidden_kernel(
         page_slots(3 * P)
         quantise_pages(1)
 
-        sums = [ps.tile([P, 2, n], F32, name=f"sum{h}", tag="wide", bufs=4) for h, n in enumerate(widths)]
-        for h, piece in enumerate(pieces):
-            for e in range(2):
+        sums = [ps.tile([P, E // P, n], F32, name=f"sum{h}", tag="bank", bufs=BANKS) for h, n in enumerate(widths)]
+        for h, piece in enumerate(PIECES):
+            for e in range(E // P):
                 cols = slice(e * P, (e + 1) * P)
                 nc.tensor.matmul_mx(
                     out=sums[h][:, e, :], lhsT=wo[:, cols].bitcast(FP8X4), lhsT_scale=wo_s[:, cols],
                     rhs=wq[:, piece].bitcast(FP8X4), rhs_scale=wq_s[:, piece], start=(e == 0), stop=False,
                 )
 
-        for h in range(len(pieces)):
+        for h in range(len(PIECES)):
             for t in range(1, PACK):
-                nc.scalar.activation(found[h][:, t, :], windows[h][t], COPY)
+                nc.scalar.activation(found[h][:, t, :], listed[h][t], COPY)
 
-        scaled = [sb.tile([P, PACK, n], BF16, name=f"scaled{h}") for h, n in enumerate(widths[:2])]
-        for t, h in [(0, 0), (0, 1), (1, 0), (2, 0), (3, 0), (1, 1), (2, 1), (3, 1)]:
+        scaled = [sb.tile([P, PACK, n], BF16, name=f"scaled{h}") for h, n in enumerate(widths[:last])]
+        gathered_order = [(h, 0) for h in range(last)] + [(h, t) for h in range(last) for t in range(1, PACK)]
+        for h, t in gathered_order:
             nc.gpsimd.tensor_scalar(scaled[h][:, t, :], found[h][:, t, :], kf2_sb[:, t : t + 1], 0.0, MULT, ADD)
 
-        for h, piece in enumerate(pieces):
+        for h, piece in enumerate(PIECES):
             n = widths[h]
             w2 = sb.tile([P, n, PACK], BF16, name=f"w2_{h}", tag=f"rounded{min(h, 1)}", align_bytes=64)
-            if h < 2:
-                nc.vector.tensor_copy(
-                    w2[:].rearrange("p (c j) t -> p c t j", j=4), scaled[h][:].rearrange("p t (c j) -> p c t j", j=4)
-                )
+            woven = w2[:].rearrange("p (c j) t -> p c t j", j=4)
+            if h < last:
+                nc.vector.tensor_copy(woven, scaled[h][:].rearrange("p t (c j) -> p c t j", j=4))
             else:
                 nc.vector.tensor_tensor(
-                    w2[:].rearrange("p (c j) t -> p c t j", j=4), found[h][:].rearrange("p t (c j) -> p c t j", j=4),
+                    woven, found[h][:].rearrange("p t (c j) -> p c t j", j=4),
                     kf2_sb[:].unsqueeze(1).unsqueeze(3).broadcast_to([P, n // 4, PACK, 4]), MULT,
                 )
             w2q = sb.tile([P, n], U32, name=f"w2q_{h}", align_bytes=64)
             w2q_s = sb.tile([P, n], U8, name=f"w2q_s_{h}", align_bytes=64)
             nc.vector.quantize_mx(out=w2q[:].bitcast(FP8X4), scales=w2q_s[:], in_=w2[:].rearrange("p n t -> p (n t)"))
-            for e in range(2):
+            for e in range(E // P):
                 cols = slice(e * P, (e + 1) * P)
                 nc.tensor.matmul_mx(
                     out=sums[h][:, e, :], lhsT=wp[:, cols].bitcast(FP4X4), lhsT_scale=wp_s[:, cols],
-                    rhs=w2q[:].bitcast(FP8X4), rhs_scale=w2q_s[:], start=False, stop=(e == 1),
+                    rhs=w2q[:].bitcast(FP8X4), rhs_scale=w2q_s[:], start=False, stop=(e == E // P - 1),
                 )
-            res = sb.tile([P, 2, n], F32, name=f"res{h}")
-            if h < 2:
+            res = sb.tile([P, E // P, n], F32, name=f"res{h}")
+            if h < last:
                 nc.scalar.copy(res[:], sums[h][:])
             else:
                 nc.vector.tensor_copy(res[:], sums[h][:])

from contextlib import ExitStack

import concourse.mybir as mybir

D, K, T, U, I, E = 512, 512, 2048, 1024, 512, 256
FLOPS = 2 * D * K * I + 2 * D * K * U + 2 * 2 * K * E * I

F32 = mybir.dt.float32
BF16 = mybir.dt.bfloat16
I32 = mybir.dt.int32
U32 = mybir.dt.uint32
U16 = mybir.dt.uint16
U8 = mybir.dt.uint8
FP8X4 = mybir.dt.float8_e4m3fn_x4
FP4X4 = mybir.dt.float4_e2m1fn_x4
COPY = mybir.ActivationFunctionType.Copy
MULT = mybir.AluOpType.mult
ADD = mybir.AluOpType.add

P = 128
PACK = 4
QUADRANTS = 4
BANK = 512
BANKS = 8
HALF = I // 2
LINE = 16
PER_COLUMN = 16
PIECES = (slice(0, 256), slice(256, 384), slice(384, 512))


def load_scales(queue, plane, scales):
    for q in range(QUADRANTS):
        queue.dma_start(
            out=plane[32 * q : 32 * q + 4, :].bitcast(I32),
            in_=scales[0, 4 * q : 4 * q + 4, :].bitcast(I32),
        )


def fill_scales(queue, plane, scales, quadrants):
    for q in quadrants:
        rows = scales[0, 4 * q : 4 * q + 4, :].bitcast(I32)
        queue.dma_start(
            out=plane[32 * q : 32 * q + 32, :].bitcast(I32),
            in_=rows.unsqueeze(0).broadcast_to([32 // 4, 4, rows.shape[1]]),
        )


def load_words(nc, tile, words):
    nc.sync.dma_start(out=tile[:].bitcast(I32), in_=words.bitcast(I32))


def deal(engine, dealt, raw, element_bytes):
    run = LINE // element_bytes
    engine.tensor_copy(
        out=dealt[:].rearrange("p (t c j) -> p c t j", t=PACK, j=run),
        in_=raw[:].rearrange("p (c j t) -> p c t j", t=PACK, j=run),
    )


def tile_attend_pagesandhidden_kernel(
    tc, pages_words, pages_scales, wa_words, wa_scales, notes_words, notes_scales, wb_words, wb_scales,
    kf, kf2, wo_words, wo_scales, wp_words, wp_scales, offs, offs2, out,
):
    nc = tc.nc
    with ExitStack() as ctx:
        sb = ctx.enter_context(tc.tile_pool(name="sb", bufs=1))
        ps = ctx.enter_context(tc.psum_pool(name="ps", bufs=1))

        wb_raw = sb.tile([P, K], U16, align_bytes=64)
        wb_s_raw = sb.tile([P, K], U8, align_bytes=64)
        notes = sb.tile([P, U], U32, align_bytes=64)
        notes_s = sb.tile([P, U], U8, align_bytes=64)
        pages = sb.tile([P, T], U16, align_bytes=64)
        pages_s = sb.tile([P, T], U8, align_bytes=64)
        wa_raw = sb.tile([P, K], U32, align_bytes=64)
        wa_s_raw = sb.tile([P, K], U8, align_bytes=64)
        wo = sb.tile([P, E], U32, align_bytes=64)
        wo_s = sb.tile([P, E], U8, align_bytes=64)
        wp = sb.tile([P, E], U16, align_bytes=64)
        wp_s = sb.tile([P, E], U8, align_bytes=64)
        list1 = sb.tile([P, I // PER_COLUMN], U16)
        list2 = sb.tile([P, I // PER_COLUMN], U16)
        kf_sb = sb.tile([P, PACK], F32)
        kf2_sb = sb.tile([P, PACK], F32)

        for plane in (pages_s, wa_s_raw, wo_s, wp_s):
            nc.vector.memset(plane[:].bitcast(I32), 0)

        fill_scales(nc.scalar, wb_s_raw, wb_scales, range(QUADRANTS))
        load_words(nc, wb_raw, wb_words[0])
        fill_scales(nc.sync, notes_s, notes_scales, range(1))
        load_words(nc, notes, notes_words[0].rearrange("p n t -> p (n t)"))
        fill_scales(nc.sync, notes_s, notes_scales, range(1, QUADRANTS))
        load_words(nc, pages, pages_words[0])
        nc.sync.dma_start(list1[:], offs)
        load_scales(nc.sync, pages_s, pages_scales)
        load_words(nc, wa_raw, wa_words[0].rearrange("p n t -> p (n t)"))
        load_scales(nc.sync, wa_s_raw, wa_scales)
        nc.sync.dma_start(list2[:], offs2)
        nc.gpsimd.dma_start(out=kf_sb[:], in_=kf.rearrange("(p t) o -> p (t o)", t=PACK))
        nc.gpsimd.dma_start(out=kf2_sb[:], in_=kf2.rearrange("(p t) o -> p (t o)", t=PACK))
        load_scales(nc.sync, wo_s, wo_scales)
        load_words(nc, wo, wo_words[0].rearrange("p n t -> p (n t)"))
        load_scales(nc.sync, wp_s, wp_scales)
        load_words(nc, wp, wp_words[0])

        wb = sb.tile([P, K], U16, align_bytes=64)
        wb_s = sb.tile([P, K], U8, align_bytes=64)
        deal(nc.vector, wb_s, wb_s_raw, 1)
        deal(nc.vector, wb, wb_raw, 2)

        h1 = [sb.tile([P, U], F32, name=f"h1_{t}") for t in range(PACK)]
        for t in range(PACK):
            cols = slice(t * P, (t + 1) * P)
            for u0 in range(0, U, BANK):
                h_bank = ps.tile([P, BANK], F32, tag="bank", bufs=BANKS)
                nc.tensor.matmul_mx(
                    out=h_bank[:], lhsT=wb[:, cols].bitcast(FP4X4), lhsT_scale=wb_s[:, cols],
                    rhs=notes[:, u0 : u0 + BANK].bitcast(FP8X4), rhs_scale=notes_s[:, u0 : u0 + BANK],
                    start=True, stop=True,
                )
                nc.scalar.activation(h1[t][:, u0 : u0 + BANK], h_bank[:], COPY)

        picked = sb.tile([P, I], U16, align_bytes=64)
        picked_s = sb.tile([P, I], U8, align_bytes=64)
        nc.vector.tensor_copy(picked[:], pages[:].indirect(list1[:]))
        nc.vector.tensor_copy(picked_s[:], pages_s[:].indirect(list1[:]))
        wa = sb.tile([P, K], U32, align_bytes=64)
        wa_s = sb.tile([P, K], U8, align_bytes=64)
        deal(nc.gpsimd, wa, wa_raw, 4)
        deal(nc.gpsimd, wa_s, wa_s_raw, 1)

        widths = [piece.stop - piece.start for piece in PIECES]
        last = len(PIECES) - 1
        found = [sb.tile([P, PACK, n], F32, name=f"found{h}") for h, n in enumerate(widths)]
        listed = [
            [h1[t][:].indirect(list2[:, piece.start // PER_COLUMN : piece.stop // PER_COLUMN]) for t in range(PACK)]
            for piece in PIECES
        ]
        for h in range(len(PIECES)):
            nc.vector.tensor_copy(found[h][:, 0, :], listed[h][0])

        wq = sb.tile([P, I], U32, align_bytes=64)
        wq_s = sb.tile([P, I], U8, align_bytes=64)
        w = [sb.tile([P, HALF, PACK], BF16, name=f"w{g}", tag=f"rounded{g}", align_bytes=64) for g in range(2)]

        def page_slots(i0):
            z_bank = ps.tile([P, PACK, P], F32, tag="bank", bufs=BANKS)
            for t in range(PACK):
                cols = slice(t * P, (t + 1) * P)
                nc.tensor.matmul_mx(
                    out=z_bank[:, t, :], lhsT=wa[:, cols].bitcast(FP8X4), lhsT_scale=wa_s[:, cols],
                    rhs=picked[:, i0 : i0 + P].bitcast(FP4X4), rhs_scale=picked_s[:, i0 : i0 + P],
                    start=True, stop=True,
                )
            nc.vector.tensor_tensor(
                w[i0 // HALF][:, i0 % HALF : i0 % HALF + P, :], z_bank[:].rearrange("p t n -> p n t"),
                kf_sb[:].unsqueeze(1).broadcast_to([P, P, PACK]), MULT,
            )

        def quantise_pages(g):
            slots = slice(g * HALF, (g + 1) * HALF)
            nc.vector.quantize_mx(
                out=wq[:, slots].bitcast(FP8X4), scales=wq_s[:, slots], in_=w[g][:].rearrange("p n t -> p (n t)")
            )

        page_slots(0)
        page_slots(P)
        page_slots(2 * P)
        quantise_pages(0)
        page_slots(3 * P)
        quantise_pages(1)

        sums = [ps.tile([P, E // P, n], F32, name=f"sum{h}", tag="bank", bufs=BANKS) for h, n in enumerate(widths)]
        for h, piece in enumerate(PIECES):
            for e in range(E // P):
                cols = slice(e * P, (e + 1) * P)
                nc.tensor.matmul_mx(
                    out=sums[h][:, e, :], lhsT=wo[:, cols].bitcast(FP8X4), lhsT_scale=wo_s[:, cols],
                    rhs=wq[:, piece].bitcast(FP8X4), rhs_scale=wq_s[:, piece], start=(e == 0), stop=False,
                )

        for h in range(len(PIECES)):
            for t in range(1, PACK):
                nc.scalar.activation(found[h][:, t, :], listed[h][t], COPY)

        scaled = [sb.tile([P, PACK, n], BF16, name=f"scaled{h}") for h, n in enumerate(widths[:last])]
        gathered_order = [(h, 0) for h in range(last)] + [(h, t) for h in range(last) for t in range(1, PACK)]
        for h, t in gathered_order:
            nc.gpsimd.tensor_scalar(scaled[h][:, t, :], found[h][:, t, :], kf2_sb[:, t : t + 1], 0.0, MULT, ADD)

        for h, piece in enumerate(PIECES):
            n = widths[h]
            w2 = sb.tile([P, n, PACK], BF16, name=f"w2_{h}", tag=f"rounded{min(h, 1)}", align_bytes=64)
            woven = w2[:].rearrange("p (c j) t -> p c t j", j=4)
            if h < last:
                nc.vector.tensor_copy(woven, scaled[h][:].rearrange("p t (c j) -> p c t j", j=4))
            else:
                nc.vector.tensor_tensor(
                    woven, found[h][:].rearrange("p t (c j) -> p c t j", j=4),
                    kf2_sb[:].unsqueeze(1).unsqueeze(3).broadcast_to([P, n // 4, PACK, 4]), MULT,
                )
            w2q = sb.tile([P, n], U32, name=f"w2q_{h}", align_bytes=64)
            w2q_s = sb.tile([P, n], U8, name=f"w2q_s_{h}", align_bytes=64)
            nc.vector.quantize_mx(out=w2q[:].bitcast(FP8X4), scales=w2q_s[:], in_=w2[:].rearrange("p n t -> p (n t)"))
            for e in range(E // P):
                cols = slice(e * P, (e + 1) * P)
                nc.tensor.matmul_mx(
                    out=sums[h][:, e, :], lhsT=wp[:, cols].bitcast(FP4X4), lhsT_scale=wp_s[:, cols],
                    rhs=w2q[:].bitcast(FP8X4), rhs_scale=w2q_s[:], start=False, stop=(e == E // P - 1),
                )
            res = sb.tile([P, E // P, n], F32, name=f"res{h}")
            if h < last:
                nc.scalar.copy(res[:], sums[h][:])
            else:
                nc.vector.tensor_copy(res[:], sums[h][:])
            nc.sync.dma_start(out=out[:, piece].rearrange("(e p) n -> p e n", p=P), in_=res[:])
